import numpy as np, ml_dtypes
CORES = [2,6,10,14,18,22,26,30]
N = 8
BF = ml_dtypes.bfloat16
def gentries(a):
    return np.ascontiguousarray(a.reshape(8, 16, -1).transpose(0, 2, 1)).reshape(8, -1)
def gtable(e):
    e = np.asarray(e); return np.ascontiguousarray(e.reshape(8, -1, 16).transpose(0, 2, 1)).reshape(128, -1).astype(np.int32)
W, NB, T, CA, LV, LI, LG = 4096, 2048, 5, 3, 9, 3, 1
P, S = NB // 16, W // (NB // 16)
def parts(rng):
    return rng.integers(0, 256, (N, 8, 16, W)), rng.integers(0, 256, (N, 8, 16, P)), rng.integers(0, 16, (N, 8, 16)), rng.integers(0, W, (N, 8, NB)), rng.integers(0, W, (N, 8, NB))
def pack(x, z, w, a, b):
    return {"xt": np.reshape(x, (N, 128, W)).astype(np.float32).astype(BF), "zp": np.reshape(z, (N, 128, P)).astype(np.float32).astype(BF), "wl": np.reshape(w, (N, 128, 1)).astype(np.float32).astype(BF),
            "ba": np.stack([gtable(v) for v in a]), "bb": np.stack([gtable(v) for v in b])}
def setup_inputs(rng):
    x, z, w, a, b = parts(rng)
    return pack(x, z, w, a, np.where(rng.random(b.shape) < 0.125, a, b))
def setup_inputs_corners(rng):
    x, z, w, a, b = parts(rng); pol = 255 * (np.arange(8) & 1)
    good = rng.random((N, 8, W)) < 0.5; good[..., W - 4:W - 1] = False
    far = np.abs(pol[None, :, None, None] - rng.integers(128, 256, x.shape))
    x = np.where(good[:, :, None, :], pol[None, :, None, None], far)
    z = np.broadcast_to(pol[None, :, None, None], z.shape).copy()
    o = np.argsort(rng.random((N, 8, 16)), axis=-1); v = rng.choice(np.array([128, 200]), (N, 8, 16))
    x[..., W - 4] = 128; x[..., W - 3] = np.where(o < LV, v, 60); x[..., W - 2] = np.where(o < LV - 1, v, 60)
    own = np.arange(NB).reshape(P, 16)
    for q in range(N):
        for g in range(8):
            pa, pb = rng.integers(0, W, 8192), rng.integers(0, W, 8192); pc = ((pa * pb >> 5) + pa + 37 * pb) & (W - 1); k = good[q, g]
            yes = np.flatnonzero(~k[pa] & ~k[pb] & k[pc] & (pa != pb)); no = np.flatnonzero((k[pa] | k[pb]) & (pa != pb))
            n = rng.choice(np.array([0, 1, CA - 1, CA, CA + 1, 16]), P); n[P - 1] = CA; n[0] = 16; n[2] = CA + 1
            m = np.argsort(rng.random((P, 16)), axis=1) < n[:, None]
            i = np.where(m, yes[rng.integers(0, len(yes), (P, 16))], no[rng.integers(0, len(no), (P, 16))]); aa, bb = pa[i], pb[i]
            kp = rng.integers(0, 12, P); kp[0] = 9; kp[P - 1] = 9; kp[2] = 9; kp[1] = 2; kp[P - 2] = 3; kp[3] = 0; kp[P - 3] = 1
            s = (kp == 0) | (kp == 2) | (kp == 3); aa[s] = own[s]; bb[s] = own[s]
            e = (W - 1) * rng.integers(0, 2, (P, 16)); aa[kp == 1] = e[kp == 1]; bb[kp == 1] = e[kp == 1]
            aa[kp == 4] = e[kp == 4]; bb[kp == 4] = W - 1 - e[kp == 4]
            slot = rng.integers(0, 16, P)
            for c, col in ((2, W - 3), (3, W - 2)):
                r = np.flatnonzero(kp == c); aa[r, slot[r]] = W - 4; bb[r, slot[r]] = col; z[q, g][:, r] = x[q, g, :, col][:, None]
            a[q, g] = aa.reshape(-1); b[q, g] = bb.reshape(-1)
    b[1] = a[1]
    w[:, 0] = 0; w[:, 1] = 15; w[:, 2] = 0; w[:, 2, 15] = 15; w[:, 3] = 15 * rng.integers(0, 2, (N, 16))
    return pack(x, z, w, a, b)
def setup_inputs_ends(rng):
    kind = rng.integers(0, 4, (N, 8, 1, W)); x = 255 * np.where(kind > 1, rng.integers(0, 2, (N, 8, 16, W)), kind)
    x = np.where((kind == 3) & (rng.random(x.shape) < 0.25), x ^ 1, x)
    hi = np.arange(8) & 1
    x[..., 0] = 255 * (1 - hi)[None, :, None]; x[..., W - 1] = 255 * hi[None, :, None]; x[0, ::2, :, W - 37] = 255
    cc = (((W - 1) * (W - 2) >> 5) + W - 1 + 37 * (W - 2)) & (W - 1)
    x[:, 1::2, :, W - 2] = 255; x[:, 1::2, :, cc] = 255
    zk = rng.integers(0, 3, (N, 8, 1, P)); z = 255 * np.where(zk == 2, rng.integers(0, 2, (N, 8, 16, P)), zk)
    w = 15 * rng.integers(0, 2, (N, 8, 16)); w[:, 1] = 15; w[:, 7] = 15; w[:, 2] = 0
    sh = (N, 8, NB)
    a = np.where(rng.random(sh) < 0.8, (W - 1) * rng.integers(0, 2, sh), rng.integers(0, W, sh))
    b = np.where(rng.random(sh) < 0.8, (W - 1) * rng.integers(0, 2, sh), rng.integers(0, W, sh))
    n = rng.integers(10, 17, (8, P, 1)); n[:, 0] = 16; n[:, P - 1] = 16
    m = (np.argsort(rng.random((8, P, 16)), axis=-1) < n).reshape(8, NB); top = ((W - 1) * hi)[:, None]
    a[0] = np.where(m, top, a[0]); b[0] = np.where(m, W - 1 - top, b[0])
    z[0] = 255 * (np.argsort(rng.random((8, 16, P)), axis=1) < rng.integers(0, 7, (8, 1, P)))
    for q in range(1, N):
        for g in (1, 7):
            for i, va, vb, vz in ((0, 0, W - 1, 255), (P - 1, 0, W - 1, 255), (1, W - 1, 0, 0), (P - 2, W - 1, 0, 0), (2, W - 1, W - 2, 0), (P - 3, W - 1, W - 2, 0)):
                a[q, g, 16 * i:16 * i + 16] = va; b[q, g, 16 * i:16 * i + 16] = vb; z[q, g, :, i] = vz
    return pack(x, z, w, a, b)
def setup_inputs_spread(rng):
    x, z, w, a, b = parts(rng)
    x = (np.exp2(8 * rng.random((N, 8, 1, W))) * rng.random(x.shape)).astype(np.int64)
    z = (np.exp2(8 * rng.random((N, 8, 1, P))) * rng.random(z.shape)).astype(np.int64)
    w = w >> rng.integers(0, 5, w.shape)
    a = (W * rng.random(a.shape) ** rng.integers(1, 5, (N, 8, 1))).astype(np.int64); b = (W * rng.random(b.shape) ** rng.integers(1, 5, (N, 8, 1))).astype(np.int64)
    return pack(x, z, w, np.minimum(a, W - 1), np.minimum(b, W - 1))
def setup_inputs_ties(rng):
    x, z, w, a, b = parts(rng)
    base = rng.integers(0, 256, (N, 8, 16, 6)); base[:, ::2] = rng.choice(np.array([0, 1, 128, 254, 255]), (N, 4, 16, 6))
    x = np.take_along_axis(base, rng.integers(0, 6, (N, 8, 1, W)), 3)
    z = np.where(rng.random((N, 8, 1, P)) < 0.75, np.take_along_axis(base, rng.integers(0, 6, (N, 8, 1, P)), 3), z)
    m = rng.random((N, 8, P, 1)) < 0.25
    a = a.reshape(N, 8, P, 16); b = b.reshape(N, 8, P, 16); b = np.where(rng.random(b.shape) < 0.125, a, b)
    a = np.where(m, a[..., :1], a).reshape(N, 8, NB); b = np.where(m, b[..., :1], b).reshape(N, 8, NB)
    return pack(x, z, w, a, b)
def check_inputs(d):
    bad = []
    for k, lo, hi in (("xt", 0, 255), ("zp", 0, 255), ("wl", 0, 15), ("ba", 0, W - 1), ("bb", 0, W - 1)):
        v = np.asarray(d[k]).astype(np.float64)
        if not np.all((v >= lo) & (v <= hi) & (v == np.floor(v))): bad.append("range of " + k)
    return bad
def reference(xt, zp, wl, ba, bb):
    X = xt.astype(np.float32).astype(np.int32).reshape(N, 8, 16, W); z = zp.astype(np.float32).astype(np.int32).reshape(N, 8, 16, P)
    w = wl.astype(np.float32).astype(np.int32).reshape(N, 8, 16, 1)
    L = [np.stack([gentries(v) for v in m]).astype(np.int32) for m in (ba, bb)]
    I = np.zeros((N, 8, NB), np.int32); G = np.zeros((N, 8, NB), np.int32); rej = [0] * N
    def before(m):
        m = m.astype(np.int32).reshape(8, P, 16)
        return (np.add.accumulate(m, axis=2) - m).reshape(8, NB)
    for t in range(T):
        now = [0] * N
        for q in range(N):
            s = (q + t) % N
            H = L[t % 2][q]; O = L[1 - t % 2][q]; C = ((H * O >> 5) + H + 37 * O) & (W - 1)
            h, o, c = [np.take_along_axis(X[s], v[:, None, :], 2) for v in (H, O, C)]
            zz = np.repeat(z[q], 16, axis=2); dh, do, dc = [np.add.reduce(np.abs(v - zz), axis=1) for v in (h, o, c)]
            live = H != O
            rec = live & (do <= np.minimum(dh, dc))
            want = live & ~rec & (dc < dh) & (G[q] < LG); am = want & (before(want) < CA)
            ins = live & ~rec & ~am
            ch = np.where(rec[:, None, :], o, np.where(am[:, None, :], c, h))
            V = np.add.reduce((ch - h).reshape(8, 16, P, 16), axis=3)
            ok = np.add.reduce((V >= 0).astype(np.int32), axis=1) >= LV
            now[s] = int(np.add.reduce((~ok).astype(np.int64), axis=None)); yes = np.repeat(ok, 16, axis=1)
            I[q] += ins | ((rec | am) & ~yes); G[q] += am & yes
            H2 = np.where(yes & rec, O, np.where(yes & am, C, H))
            sp = I[q] >= LI; v = np.where((before(sp) & 1) == 1, C, H)
            H2 = np.where(sp, v, H2); O2 = np.where(sp, v, O); I[q] = np.where(sp, 0, I[q])
            M = np.maximum.reduce(ch.reshape(8, 16, P, 16), axis=3); u = np.add.reduce(w[s] * M, axis=1) & (W - 1)
            O2 = np.where(live, O2, ((H * np.repeat(u, 16, axis=1) >> 5) + H + rej[s]) & (W - 1))
            L[t % 2][q] = H2; L[1 - t % 2][q] = O2
            if t < T - 1:
                z[q] = np.abs(z[q] - M)
                at = (S * np.arange(P)[None, :] + (u & (S - 1)))[:, None, :]
                np.put_along_axis(X[s], at, (np.take_along_axis(X[s], at, 2) + M) >> 1, 2)
        rej = now
    home = [(s - (T - 1)) % N for s in range(N)]
    ya, yb, yi, yg = [np.stack([gtable(m[q]) for q in home]).astype(np.float32) for m in (L[0], L[1], I, G)]
    return {"ya": ya, "yb": yb, "yi": yi, "yg": yg}

@@ -1,0 +1,533 @@
+import numpy as np
+from concourse.mybir import AluOpType as OP, ActivationFunctionType as AF
+
+NT = 5
+NH = 2
+NPK = 64
+NB = 16 * NPK
+NPC = 2
+PCB = NB // NPC
+PCK = NPK // NPC
+
+SCRATCH = {"X": ("sbuf", [128, 4096], "bfloat16"), "ia": ("sbuf", [128, 128], "int32"), "ib": ("sbuf", [128, 128], "int32"),
+           "wc": ("sbuf", [128, 1], "bfloat16"), "r32": ("sbuf", [128, 1], "float32"), "ri": ("sbuf", [128, 1], "int32"),
+           "rj": ("sbuf", [128, 1], "int32"), "mi": ("sbuf", [128, 64], "int32"), "mj": ("sbuf", [128, 64], "int32"),
+           "base0": ("sbuf", [128, 64], "float32"), "Q": ("sbuf", [128, 144], "bfloat16"),
+           "zmask": ("sbuf", [128, NB], "bfloat16"), "K32": ("sbuf", [128, NT], "float32"), "ks": ("sbuf", [128, 2 * NT], "float32"),
+           "SI": ("sbuf", [128, 256], "float32")}
+F32 = ("P", "dhs", "dos", "thr", "m", "t2", "cho", "um", "sc", "P2", "ad", "hsb", "spoh", "kset", "absoh")
+I32 = ("S", "ci", "ui", "u12", "u5", "gx", "gs", "S2", "fx", "pc", "od2")
+SMALL = {}
+for _n in ("ones", "bt", "BM", "I", "nI", "n8I", "I2", "n3I", "TRI", "TRI16", "Wb", "cm"):
+    SCRATCH[_n] = ("sbuf", [128, 128], "bfloat16")
+for _n in ("If", "nIf", "If32", "If1184", "o16f"):
+    SCRATCH[_n] = ("sbuf", [128, 128], "float32")
+for _t in range(NT):
+    SCRATCH["L%d" % _t] = ("sbuf", [128, 256], "float32")
+    SCRATCH["Z%d" % _t] = ("sbuf", [128, 384], "bfloat16")
+    SCRATCH["SL%d" % _t] = ("sbuf", [128, 256], "float32")
+    SCRATCH["SZ%d" % _t] = ("sbuf", [128, 384], "bfloat16")
+for _h in range(NH):
+    for _n in ("zbuf", "zexp", "hr", "ha", "od", "orl", "cd", "cabs", "ch", "Mf"):
+        SCRATCH["%s_%d" % (_n, _h)] = ("sbuf", [128, NB], "bfloat16")
+    SCRATCH["ho16_%d" % _h] = ("sbuf", [128, 128], "uint16")
+    for _n in ("c16", "ch16"):
+        SCRATCH["%s_%d" % (_n, _h)] = ("sbuf", [128, 64], "uint16")
+    SCRATCH["u16_%d" % _h] = ("sbuf", [128, 4], "uint16")
+    for _i, _n in enumerate(F32):
+        SMALL["%s_%d" % (_n, _h)] = ("F_%d" % _h, 64 * _i)
+    SCRATCH["F_%d" % _h] = ("sbuf", [128, 64 * len(F32)], "float32")
+    for _i, _n in enumerate(I32):
+        SMALL["%s_%d" % (_n, _h)] = ("J_%d" % _h, 64 * _i)
+    SCRATCH["J_%d" % _h] = ("sbuf", [128, 64 * len(I32)], "int32")
+    for _n in ("set", "rec", "w", "am", "yv", "acc", "inc", "sp", "dm"):
+        SCRATCH["%s_%d" % (_n, _h)] = ("sbuf", [128, 64], "bfloat16")
+for _b in range(8):
+    SCRATCH["ps%d" % _b] = ("psum", [128, 512], "float32")
+
+SEMAPHORES = ["qv", "qa", "qt", "qg", "loc"] + ["in%d" % _i for _i in range(7)] + ["out%d" % _i for _i in range(8)] + \
+    ["arr_%d_%d_%s" % (_t, _h, _k) for _t in range(1, NT) for _h in range(NH) for _k in "LZN"]
+
+PS = {}
+for _h in range(NH):
+    for _i, _n in enumerate(("dh", "do", "dc", "dhp", "V", "cnt", "cntv", "u")):
+        PS[_n, _h] = (2 + _h, _i)
+    for _i, _n in enumerate(("H", "L", "OH", "L2", "Hn", "zd", "cnt2", "hsum")):
+        PS[_n, _h] = (4 + _h, _i)
+    for _i, _n in enumerate(("CH", "d", "tmp")):
+        PS[_n, _h] = (6, 3 * _h + _i)
+    for _i, _n in enumerate(("incs", "Gs", "In", "I2")):
+        PS[_n, _h] = (7, 4 * _h + _i)
+PS["mask", 0] = (6, 6)
+
+CY = 0.83e-3 * 1.25
+PCY = 0.5e-3
+GA = 1.6
+BONUS, WINDOW = 2.0, 0.03
+OFFS = {}
+HOP = 3.5
+
+
+def build():
+    ops = []
+    cur = {"h": None, "t": -1}
+
+    def add(q, cost, fn, r, w, **kw):
+        ops.append(dict(q=q, cost=cost, fn=fn, r=list(r), w=list(w), h=cur["h"], t=cur["t"], **kw))
+
+    def ps(name, h, T):
+        b, i = PS[name, h]
+        return T["ps%d" % b][:, 64 * i:64 * i + 64]
+
+    def full(name):
+        return (name, lambda T: T[name][:])
+
+    def pk(name, h):
+        return ("ps%d:%s%d" % (PS[name, h][0], name, h), lambda T: ps(name, h, T))
+
+    def sb(name, h):
+        n = "%s_%d" % (name, h)
+        if n in SMALL:
+            b, c = SMALL[n]
+            return (n, lambda T: T[b][:, c:c + 64])
+        return (n, lambda T: T[n][:])
+
+    def cols(name, a, b, step=1, key=None):
+        return (key or name, lambda T: T[name][:, a:b:step] if step != 1 else T[name][:, a:b])
+
+    def inps(x):
+        return x[0].startswith("ps")
+
+    def tt(out, a, b, op, n=64):
+        c = max(64, n * (1 if inps(a) or inps(b) else 2))
+        add("v", c * CY, lambda g, T: g.vector.tensor_tensor(out[1](T), a[1](T), b[1](T), op), [a[0], b[0]], [out[0]])
+
+    def ts(out, a, s1, op0, s2=None, op1=None, n=64, half=False, extra=()):
+        c = max(64, n * (0.5 if half else 1))
+
+        def fn(g, T):
+            sc = s1(T) if callable_(s1) else s1
+            if op1 is None:
+                return g.vector.tensor_scalar(out[1](T), a[1](T), sc, None, op0)
+            return g.vector.tensor_scalar(out[1](T), a[1](T), sc, s2, op0, op1)
+        add("v", c * CY, fn, [a[0]] + list(extra), [out[0]])
+
+    def callable_(x):
+        return not isinstance(x, (int, float))
+
+    def cp(out, a, n=64):
+        add("v", max(64, n) * CY, lambda g, T: g.vector.tensor_copy(out[1](T), a[1](T)), [a[0]], [out[0]])
+
+    def act(out, a, func, scale=1.0, bias=0.0, n=64, extra=(), accum=None):
+        def fn(g, T):
+            kw = {}
+            if scale != 1.0 or callable_(scale):
+                kw["scale"] = scale(T) if callable_(scale) else scale
+            if bias != 0.0:
+                kw["bias"] = bias
+            if accum is not None:
+                kw["accum_out"] = accum[1](T)
+            return g.scalar.activation(out[1](T), a[1](T), func, **kw)
+        add("a", max(64, n) * CY + 0.02, fn, [a[0]] + list(extra), [out[0]] + ([accum[0]] if accum is not None else []))
+
+    def mm(out, terms):
+        def fn(g, T):
+            r = None
+            for k, (l, x, n, f) in enumerate(terms):
+                r = g.tensor.matmul(out[1](T), l[1](T), x[1](T), k == 0, k == len(terms) - 1)
+            return r
+        keys = []
+        for l, x, n, f in terms:
+            for y in (l, x):
+                for kk in (y[0] if isinstance(y[0], (list, tuple)) else [y[0]]):
+                    if kk not in keys:
+                        keys.append(kk)
+        add("t", sum(max(64, n) * f for l, x, n, f in terms) * PCY, fn, keys, [out[0]])
+
+    def f1(l, x, n=64):
+        return (full(l), x, n, 1)
+
+    def f4(l, x, n=64):
+        return (full(l), x, n, 4)
+
+    def gather_v(out, lst, z, n):
+        add("v", 0.05 + n * GA * CY, lambda g, T: g.vector.tensor_tensor(out[1](T), T.X[:, 0:4096].indirect(lst[1](T)), z[1](T), OP.subtract),
+            ["X0", "X1", lst[0], z[0]], [out[0]])
+
+    def gather_a(out, lst, n):
+        add("a", 0.065 + n * GA * CY, lambda g, T: g.scalar.activation(out[1](T), T.X[:, 0:4096].indirect(lst[1](T)), AF.Copy),
+            ["X0", "X1", lst[0]], [out[0]])
+
+    def memset(name, val, n, sl=None, key=None):
+        add("v", max(64, n) * CY, lambda g, T: g.vector.memset(sl(T) if sl is not None else T[name][:], val), [], [key or name])
+
+    def dma(q, sem, out, src, cost):
+        def fn(g, T):
+            return (g.sync if q == "s" else g.scalar).dma_start(out[1](T), src[1](T))
+        add(q, 0.1, fn, [src[0]] if src[0] else [], [out[0]], sem=sem, lat=cost)
+
+    def piece(name, h, p):
+        n = "%s_%d" % (name, h)
+        return ("%s.%d" % (n, p), lambda T: T[n][:, p * PCB:(p + 1) * PCB])
+
+    def col16(name, h, j):
+        n = "%s_%d" % (name, h)
+        return (["%s.%d" % (n, p) for p in range(NPC)], lambda T: T[n][:, j:NB:16])
+
+    dma("s", "in0", full("ia"), (None, lambda T: T.ba[:]), 2.0)
+    dma("a", "in1", full("ib"), (None, lambda T: T.bb[:]), 2.0)
+    dma("s", "in2", ("X0", lambda T: T.X[:, 0:2048]), (None, lambda T: T.xt[:, 0:2048]), 5.0)
+    dma("a", "in3", ("X1", lambda T: T.X[:, 2048:4096]), (None, lambda T: T.xt[:, 2048:4096]), 5.0)
+    for h in range(NH):
+        dma("s", "in%d" % (4 + h), cols("Z0", 192 * h, 192 * h + 64, key="z0_%d" % h), (None, lambda T, h=h: T.zp[:, 64 * h:64 * h + 64]), 2.2)
+    dma("s", "in6", full("wc"), (None, lambda T: T.wl[:]), 2.2)
+    gp = lambda fn, r, w: add("g", 0.5, fn, r, w, sem="qg")
+    memset("ones", 1.0, 128)
+    gp(lambda g, T: g.affine_select(T.I[:], T.ones[:], [[-1, 128]], OP.is_equal, 0.0, 0, 1), ["ones"], ["I"])
+    act(full("If"), full("I"), AF.Copy, n=128)
+    act(full("nIf"), full("I"), AF.Copy, scale=-1.0, n=128)
+    act(full("If32"), full("I"), AF.Copy, scale=32.0, n=128)
+    act(full("If1184"), full("I"), AF.Copy, scale=1184.0, n=128)
+    memset("cm", -65536.0, 128)
+    gp(lambda g, T: g.affine_select(T.bt[:], T.ones[:], [[-16, 8], [0, 16]], OP.is_ge, 0.0, 0, 1), ["ones"], ["bt"])
+    gp(lambda g, T: g.affine_select(T.BM[:], T.bt[:], [[16, 8], [0, 16]], OP.is_ge, 0.0, 15, -1), ["bt"], ["BM"])
+    gp(lambda g, T: g.affine_select(T.TRI[:], T.BM[:], [[1, 128]], OP.is_gt, 0.0, 0, -1), ["BM"], ["TRI"])
+    for h in range(NH):
+        memset("zbuf_%d" % h, 0.0, NB // 2)
+        memset("Z0", 0.0, 64, sl=lambda T, h=h: T.Z0[:, 192 * h + 64:192 * h + 192], key="ig0_%d" % h)
+    memset("zmask", 1.0, NB // 2)
+    memset("zmask", 0.0, 64, sl=lambda T: T.zmask[:, 0:NB:16])
+    ops[-1]["r"].append("zmask")
+    memset("Q", 0.0, 144)
+    add("v", 64 * CY, lambda g, T: g.vector.tensor_copy(T.Q[:, 15:143:16], T.BM[:, 0:128:16]), ["BM", "Q"], ["Q"])
+    act(full("nI"), full("I"), AF.Copy, scale=-1.0, n=128)
+    act(full("n8I"), full("I"), AF.Copy, scale=-8192.0, n=128)
+    ts(full("TRI16"), full("I"), -16.0, OP.mult, n=128, half=True)
+    tt(full("TRI16"), full("TRI16"), full("TRI"), OP.add, n=128)
+    act(full("I2"), full("I"), AF.Copy, scale=2.0, n=128)
+    act(full("n3I"), full("I"), AF.Copy, scale=-3.0, n=128)
+    ts(full("Wb"), full("BM"), lambda T: T.wc[:], OP.mult, n=128, half=True, extra=["wc"])
+    gp(lambda g, T: g.iota(T.mi[:], [[-1, 64]], 64, 1), [], ["mi"])
+    gp(lambda g, T: g.iota(T.ri[:], [[0, 1]], 0, 1), [], ["ri"])
+    gp(lambda g, T: g.iota(T.base0[:], [[512, 4], [0, 16]], 0, 0, allow_small_or_imprecise_dtypes=True), [], ["base0"])
+    ts(full("mj"), full("mi"), 15, OP.bitwise_and)
+    ts(pk("mask", 0), full("mj"), 0.0, OP.is_equal)
+    ts(full("rj"), full("ri"), 15, OP.bitwise_and)
+    ts(full("r32"), full("rj"), 32.0, OP.mult)
+    memset("o16f", 0.0625, 128)
+
+    for h in range(NH):
+        cp(cols("L0", 128 * h, 128 * h + 64, key="l0_%d" % h), cols("ia", 64 * h, 64 * h + 64))
+        cp(cols("L0", 128 * h + 64, 128 * h + 128, key="l0_%d" % h), cols("ib", 64 * h, 64 * h + 64))
+
+    for t in range(NT):
+        last = t == NT - 1
+        scat = []
+        for h in range(NH):
+            cur["h"], cur["t"] = h, t
+            lk, zk, ik = "l%d_%d" % (t, h), "z%d_%d" % (t, h), "ig%d_%d" % (t, h)
+            ca, cb = 128 * h + 64 * (t % 2), 128 * h + 64 * (1 - t % 2)
+            LH, LO = cols("L%d" % t, ca, ca + 64, key=lk), cols("L%d" % t, cb, cb + 64, key=lk)
+            z = cols("Z%d" % t, 192 * h, 192 * h + 64, key=zk)
+            Iold = cols("Z%d" % t, 192 * h + 64, 192 * h + 128, key=ik)
+            Gold = cols("Z%d" % t, 192 * h + 128, 192 * h + 192, key=ik)
+            if t == 0:
+                cm_ = [(full("cm"), cols("ones", 0, 64), 64, 1)]
+            if t > 0:
+                add(None, 0.0, None, ["send_%d_%d_L" % (t - 1, h)], [lk], arr="arr_%d_%d_L" % (t, h), lat=HOP)
+                add(None, 0.0, None, ["send_%d_%d_Z" % (t - 1, h)], [zk], arr="arr_%d_%d_Z" % (t, h), lat=HOP)
+                add(None, 0.0, None, ["send_%d_%d_N" % (t - 1, h)], [ik], arr="arr_%d_%d_N" % (t, h), lat=HOP)
+            cp(sb("ho16", h), cols("L%d" % t, 128 * h, 128 * h + 128, key=lk), n=128)
+            add("a", 64 * CY, lambda g, T, h=h, z=z: g.scalar.activation(T["zbuf_%d" % h][:, 0:NB:16], z[1](T), AF.Copy), [zk, "zbuf_%d" % h], ["zbuf_%d" % h])
+            mm(pk("H", h), [f4("If", LH)])
+            mm(pk("L", h), [f4("If32", LH), f4("If1184", LO)] + cm_)
+            mm(pk("OH", h), [f4("If", LO), f4("nIf", LH)])
+            tt(sb("P", h), LO, pk("H", h), OP.mult)
+            tt(sb("S", h), sb("P", h), pk("L", h), OP.add)
+            ts(sb("ci", h), sb("S", h), 5, OP.arith_shift_right, 4095, OP.bitwise_and)
+            cp(sb("c16", h), sb("ci", h))
+            act(sb("absoh", h), pk("OH", h), AF.Abs)
+            act(sb("set", h), sb("absoh", h), AF.Relu, scale=-1.0, bias=1.0)
+            for p in range(NPC):
+                ze = piece("zexp", h, p)
+                add("v", PCB / 2 * CY, lambda g, T, h=h, p=p: g.vector.tensor_tensor_scan(
+                    T["zexp_%d" % h][:, p * PCB:(p + 1) * PCB], T.zmask[:, 0:PCB], T["zbuf_%d" % h][:, p * PCB:(p + 1) * PCB], 0.0, OP.mult, OP.add),
+                    ["zmask", "zbuf_%d" % h], [ze[0]])
+            lst = lambda name, a, h=h: (lambda p: ("%s_%d" % (name, h), lambda T: T["%s_%d" % (name, h)][:, a + p * PCK:a + (p + 1) * PCK]))
+            lh, lo, lc, lch = lst("ho16", 64 * (t % 2)), lst("ho16", 64 * (1 - t % 2)), lst("c16", 0), lst("ch16", 0)
+            for p in range(NPC):
+                gather_a(piece("hr", h, p), lh(p), PCB)
+                yb = ("ps%d:y" % p, lambda T, p=p: T["ps%d" % p][:, 0:PCB])
+                mm(yb, [f1("I", piece("hr", h, p), PCB), f1("nI", piece("zexp", h, p), PCB)])
+                act(piece("ha", h, p), yb, AF.Abs, n=PCB)
+            for p in range(NPC):
+                gather_v(piece("od", h, p), lo(p), piece("zexp", h, p), PCB)
+                ts(piece("orl", h, p), piece("od", h, p), 0.0, OP.min, -2.0, OP.mult, n=PCB, half=True)
+            for p in range(NPC):
+                gather_v(piece("cd", h, p), lc(p), piece("zexp", h, p), PCB)
+                act(piece("cabs", h, p), piece("cd", h, p), AF.Abs, n=PCB)
+            q = lambda j: ("Q", lambda T, j=j: T.Q[:, 15 - j:143 - j])
+            mm(pk("dh", h), [(q(j), col16("ha", h, j), 64, 1) for j in range(16)])
+            mm(pk("do", h), [(q(j), col16(n, h, j), 64, 1) for n in ("od", "orl") for j in range(16)])
+            mm(pk("dc", h), [(q(j), col16("cabs", h, j), 64, 1) for j in range(16)])
+            act(sb("dhs", h), pk("dh", h), AF.Copy)
+            act(sb("dos", h), pk("do", h), AF.Copy)
+            mm(pk("dhp", h), [f4("If", sb("dhs", h)), f1("n8I", Gold), f1("n8I", sb("set", h))])
+            tt(sb("thr", h), sb("dos", h), pk("dhp", h), OP.min)
+            tt(sb("w", h), pk("dc", h), sb("thr", h), OP.is_lt)
+            mm(pk("cnt", h), [f1("TRI16", sb("w", h))])
+            tt(sb("m", h), sb("dhs", h), pk("dc", h), OP.min)
+            tt(sb("rec", h), pk("do", h), sb("m", h), OP.is_le)
+            tt(pk("CH", h), sb("ci", h), pk("H", h), OP.subtract)
+            tt(pk("tmp", h), sb("rec", h), pk("OH", h), OP.mult)
+            ts(sb("am", h), pk("cnt", h), -13.0, OP.is_lt)
+            tt(sb("t2", h), sb("am", h), pk("CH", h), OP.mult)
+            tt(pk("d", h), sb("t2", h), pk("tmp", h), OP.add)
+            tt(sb("cho", h), LH, pk("d", h), OP.add)
+            cp(sb("ch16", h), sb("cho", h))
+            for p in range(NPC):
+                gather_a(piece("ch", h, p), lch(p), PCB)
+                add("v", PCB / 2 * CY, lambda g, T, h=h, p=p: g.vector.tensor_tensor_scan(
+                    T["Mf_%d" % h][:, p * PCB:(p + 1) * PCB], T.zmask[:, 0:PCB], T["ch_%d" % h][:, p * PCB:(p + 1) * PCB], 0.0, OP.mult, OP.max),
+                    ["zmask", "ch_%d.%d" % (h, p)], ["Mf_%d.%d" % (h, p)])
+            M = (["Mf_%d.%d" % (h, p) for p in range(NPC)], lambda T, h=h: T["Mf_%d" % h][:, 15:NB:16])
+            mm(pk("u", h), [f1("Wb", M)])
+            cp(sb("ui", h), pk("u", h))
+            if not last:
+                ts(sb("u5", h), sb("ui", h), 31, OP.bitwise_and)
+                tt(sb("um", h), sb("u5", h), pk("mask", 0), OP.mult)
+                add("v", 64 * CY, lambda g, T, sc=sb("sc", h)[1], um=sb("um", h)[1]: g.vector.tensor_tensor_scan(
+                    sc(T), T.base0[:], um(T), 0.0, OP.max, OP.add), ["base0", "um_%d" % h], ["sc_%d" % h])
+                fb, fc = SMALL["sc_%d" % h]
+                ts(sb("u16", h), ("sc_%d" % h, lambda T, fb=fb, fc=fc: T[fb][:, fc + 15:fc + 64:16]), lambda T: T.r32[:], OP.add, extra=["r32"])
+                win = lambda T, h=h: T.X[:, 2048 * h:2048 * h + 2048].indirect(T["u16_%d" % h][:, 0:4])
+                add("v", 0.05 + 64 * GA * CY, lambda g, T, gx=sb("gx", h)[1], win=win, M=M: g.vector.tensor_tensor(gx(T), win(T), M[1](T), OP.add),
+                    ["X%d" % h, "u16_%d" % h] + M[0], ["gx_%d" % h])
+                ts(sb("gs", h), sb("gx", h), 1, OP.arith_shift_right)
+                scat.append(("v", 0.05 + 64 * 4 * CY, lambda g, T, gs=sb("gs", h)[1], win=win: g.vector.tensor_copy(win(T), gs(T)),
+                             ["gs_%d" % h, "u16_%d" % h, "X%d" % h], ["X%d" % h]))
+            mm(pk("hsum", h), [(full("I"), col16("hr", h, j), 64, 1) for j in range(16)])
+            act(sb("hsb", h), pk("hsum", h), AF.Copy)
+            mm(pk("V", h), [(full("I"), col16("ch", h, j), 64, 1) for j in range(16)])
+            tt(sb("yv", h), pk("V", h), sb("hsb", h), OP.is_ge)
+            mm(pk("cntv", h), [f1("BM", sb("yv", h))])
+            ts(sb("acc", h), pk("cntv", h), 9.0, OP.is_ge)
+            mm(pk("incs", h), [f1("I", sb("rec", h)), f1("I", sb("am", h)), f1("I2", sb("set", h)), f1("I", sb("acc", h))])
+            ts(sb("inc", h), pk("incs", h), 2.0, OP.is_lt)
+            mm(pk("In", h), [f1("I", Iold), f1("I", sb("inc", h))])
+            ts(sb("sp", h), pk("In", h), 3.0, OP.is_ge)
+            mm(pk("cnt2", h), [f1("TRI", sb("sp", h))])
+            sl, sz = "SL%d" % t, "SZ%d" % t
+            sh = "send_%d_%d" % (t, h)
+            tt(pk("tmp", h), sb("set", h), pk("H", h), OP.mult)
+            ts(sb("u12", h), sb("ui", h), 4095, OP.bitwise_and)
+            tt(sb("P2", h), sb("u12", h), pk("tmp", h), OP.mult)
+            tt(sb("spoh", h), sb("sp", h), pk("OH", h), OP.mult)
+            tt(pk("CH", h), sb("sp", h), pk("CH", h), OP.mult)
+            cp(sb("pc", h), pk("cnt2", h))
+            ts(sb("od2", h), sb("pc", h), 1, OP.bitwise_and)
+            tt(pk("CH", h), sb("od2", h), pk("CH", h), OP.mult)
+            tt(pk("tmp", h), pk("CH", h), sb("spoh", h), OP.subtract)
+            tt(pk("d", h), sb("acc", h), pk("d", h), OP.mult)
+            terms = [f4("If32", LO)]
+            if t > 0:
+                act(sb("kset", h), sb("set", h), AF.Identity, scale=lambda T, t=t: T.K32[:, t - 1:t], extra=["K32.%d" % (t - 1)])
+                terms.append(f4("If", sb("kset", h)))
+            mm(pk("L2", h), terms + cm_)
+            tt(sb("S2", h), sb("P2", h), pk("L2", h), OP.add)
+            ts(sb("fx", h), sb("S2", h), 5, OP.arith_shift_right, 4095, OP.bitwise_and)
+            tt(cols(sl, cb, cb + 64, key=sh + "_lo"), sb("fx", h), pk("tmp", h), OP.add)
+            tt(sb("ad", h), LH, pk("d", h), OP.add)
+            tt(cols(sl, ca, ca + 64, key=sh + "_lh"), sb("ad", h), pk("CH", h), OP.add)
+            mm(pk("I2", h), [f1("I", Iold), f1("I", sb("inc", h)), f1("n3I", sb("sp", h))])
+            mm(pk("Gs", h), [f1("I", sb("am", h)), f1("I", sb("acc", h)), f1("I2", Gold)])
+            if last:
+                act(cols("SI", 128 * h, 128 * h + 64, key="si%d" % h), pk("I2", h), AF.Copy)
+                ts(cols("SI", 128 * h + 64, 128 * h + 128, key="sg%d" % h), pk("Gs", h), 2.0, OP.is_ge)
+                ka, kb = sh + "_lh", sh + "_lo"
+                dma("s", "out%d" % (4 * h), (None, lambda T, h=h: T.yi[:, 64 * h:64 * h + 64]), cols("SI", 128 * h, 128 * h + 64, key="si%d" % h), 2.0)
+                dma("s", "out%d" % (4 * h + 1), (None, lambda T, h=h: T.yg[:, 64 * h:64 * h + 64]), cols("SI", 128 * h + 64, 128 * h + 128, key="sg%d" % h), 2.0)
+                dma("s", "out%d" % (4 * h + 2), (None, lambda T, h=h: T.ya[:, 64 * h:64 * h + 64]), cols(sl, ca, ca + 64, key=ka), 2.0)
+                dma("s", "out%d" % (4 * h + 3), (None, lambda T, h=h: T.yb[:, 64 * h:64 * h + 64]), cols(sl, cb, cb + 64, key=kb), 2.0)
+            else:
+                act(cols(sz, 192 * h + 64, 192 * h + 128, key=sh + "_zi"), pk("I2", h), AF.Copy)
+                ts(cols(sz, 192 * h + 128, 192 * h + 192, key=sh + "_zg"), pk("Gs", h), 2.0, OP.is_ge)
+                mm(pk("zd", h), [f1("I", z), f1("nI", M)])
+                act(cols(sz, 192 * h, 192 * h + 64, key=sh + "_zz"), pk("zd", h), AF.Abs)
+                act(sb("dm", h), sb("acc", h), AF.Copy, accum=cols("ks", 2 * t + h, 2 * t + h + 1, key="ks%d_%d" % (t, h)))
+                add("g", 0.3, None, [sh + "_zz"], [sh + "_Z"], send=(t, h, "Z"))
+                add("g", 0.3, None, [sh + "_zi", sh + "_zg"], [sh + "_N"], send=(t, h, "N"))
+                add("g", 0.3, None, [sh + "_lo", sh + "_lh"], [sh + "_L"], send=(t, h, "L"))
+        for x in scat:
+            add(*x)
+        if not last:
+            kp = ("ps4:zd0", lambda T: T.ps4[:, 320:321])
+            mm(kp, [f4("o16f", cols("ks", 2 * t + h, 2 * t + h + 1, key="ks%d_%d" % (t, h)), 1) for h in range(NH)])
+            act(cols("K32", t, t + 1, key="K32.%d" % t), kp, AF.Copy, scale=-32.0, bias=32768.0)
+    return ops
+
+
+def opclass(o):
+    c = o["w"][0] if o["w"] else ""
+    for p in ("l", "z", "ig", "send_", "K32.", "ks"):
+        if o["t"] >= 0 and c.startswith(p + str(o["t"])):
+            c = p + c[len(p) + 1:]
+    return c
+
+
+def graph():
+    ops = build()
+    n = len(ops)
+    deps = [set() for _ in range(n)]
+    lastw, readers = {}, {}
+
+    def keys(l):
+        out = []
+        for k in l:
+            out += keys(k) if isinstance(k, (list, tuple)) else ([k] if k else [])
+        return out
+    for i, o in enumerate(ops):
+        o["r"], o["w"] = keys(o["r"]), keys(o["w"])
+        for k in o["r"]:
+            if k in lastw:
+                deps[i].add(lastw[k])
+        for k in o["w"]:
+            if k in lastw:
+                deps[i].add(lastw[k])
+            deps[i].update(readers.get(k, ()))
+        for k in o["r"]:
+            readers.setdefault(k, []).append(i)
+        for k in o["w"]:
+            lastw[k] = i
+            readers[k] = []
+        deps[i].discard(i)
+        o["banks"] = sorted(set(k.split(":")[0] for k in o["r"] + o["w"] if k.startswith("ps")))
+        o["cls"] = opclass(o)
+    succ = [[] for _ in range(n)]
+    for i in range(n):
+        for j in deps[i]:
+            succ[j].append(i)
+    pri = [0.0] * n
+    for i in range(n - 1, -1, -1):
+        o = ops[i]
+        pri[i] = o["cost"] + o.get("lat", 0.0) + 0.08 + max([pri[s] for s in succ[i]] or [0.0])
+    return ops, deps, succ, pri
+
+
+def schedule(gr, offs, bonus, window):
+    ops, deps, succ, pri = gr
+    n = len(ops)
+    deps = [set(d) for d in deps]
+    pri = [pri[i] + (bonus if ops[i]["h"] == 0 else 0.0) + offs.get(ops[i]["cls"], 0.0) for i in range(n)]
+    left = [len(d) for d in deps]
+    end = [0.0] * n
+    free, bank, order = {}, {}, []
+    rdy = {}
+    for i in range(n):
+        if left[i] == 0:
+            rdy[i] = 0.0
+    while rdy:
+        est, mins = {}, {}
+        for i, s in rdy.items():
+            o = ops[i]
+            q = o["q"]
+            f = free.get(q, 0.0) if q else 0.0
+            if f > s:
+                s = f
+            for b in o["banks"]:
+                for e, j in bank.get(b, {}).items():
+                    if e != q and end[j] + 0.1 > s:
+                        s = end[j] + 0.1
+            est[i] = s
+            if s < mins.get(q, 1e9):
+                mins[q] = s
+        q = min(mins, key=lambda k: mins[k])
+        i = max([k for k in est if ops[k]["q"] == q and est[k] <= mins[q] + window], key=lambda k: pri[k])
+        o, s = ops[i], est[i]
+        for b in o["banks"]:
+            for e, j in bank.get(b, {}).items():
+                if e != q:
+                    deps[i].add(j)
+            bank.setdefault(b, {})[q] = i
+        if q:
+            free[q] = s + o["cost"]
+        end[i] = s + o["cost"] + o.get("lat", 0.0)
+        o["start"] = s
+        order.append(i)
+        del rdy[i]
+        for k in succ[i]:
+            left[k] -= 1
+            if left[k] == 0:
+                rdy[k] = max(end[j] + (0.05 if ops[j]["q"] == ops[k]["q"] else 0.1) for j in deps[k])
+    assert len(order) == n
+    return deps, order, max(end)
+
+
+def plan(offs=None, bonus=None, window=None):
+    gr = graph()
+    ops = gr[0]
+    deps, order, span = schedule(gr, OFFS if offs is None else offs, BONUS if bonus is None else bonus, WINDOW if window is None else window)
+    count = {}
+    for i in order:
+        o = ops[i]
+        if o.get("sem", "").startswith(("in", "out")):
+            o["ev"] = (o["sem"], 16)
+        elif "arr" in o:
+            o["ev"] = (o["arr"], None)
+        elif "send" in o:
+            o["ev"] = None
+        else:
+            s = "q" + o["q"]
+            count[s] = count.get(s, 0) + 1
+            o["ev"] = (s, count[s])
+    return ops, deps, order, count, span
+
+
+_PLAN = []
+
+
+def rank_program(g, core, T, topo):
+    rank = T.rank_of(core)
+    if rank is None:
+        return
+    if not _PLAN:
+        _PLAN.append(plan())
+    ops, deps, order, count, _ = _PLAN[0]
+    n = len(T.cores)
+    nxt, prv = T.cores[(rank + 1) % n], T.cores[(rank - 1) % n]
+
+    def engines(a, b):
+        return topo.engines(a, b)
+    mask = topo.mask(core, nxt)
+    n_in, n_out = len(engines(prv, core)), len(engines(core, nxt))
+    rid, pid = topo.addr(nxt)[:2]
+    queues = {"v": g.vector, "a": g.scalar, "t": g.tensor, "g": g, "s": g.sync}
+    seen = {}
+    sent = 0
+    for i in order:
+        o = ops[i]
+        if o["q"] is None:
+            continue
+        q = queues[o["q"]]
+        need = {}
+        for j in deps[i]:
+            ev = ops[j]["ev"]
+            if ev is not None:
+                need[ev[0]] = max(need.get(ev[0], 0), n_in if ev[1] is None else ev[1])
+        for s in sorted(need):
+            if seen.get((o["q"], s), 0) < need[s]:
+                q.wait_ge(T.sem[s], need[s])
+                seen[o["q"], s] = need[s]
+        if "send" in o:
+            t, h, k = o["send"]
+            a, b, w = {"L": (128 * h, 128 * h + 128, "L"), "Z": (192 * h, 192 * h + 64, "Z"), "N": (192 * h + 64, 192 * h + 192, "Z")}[k]
+            g.remote_dma(T["%s%d" % (w, t + 1)][:, a:b], T["S%s%d" % (w, t)][:, a:b], T.sem["arr_%d_%d_%s" % (t + 1, h, k)], T.sem.loc, pid, rid, mask)
+            sent += n_out
+            continue
+        r = o["fn"](g, T)
+        r.then_inc(T.sem[o["ev"][0]], 16 if o["ev"][0].startswith(("in", "out")) else 1)
+    for s in sorted(count):
+        g.wait_ge(T.sem[s], count[s])
+    for k in range(8):
+        g.wait_ge(T.sem["out%d" % k], 16)
+    g.wait_ge(T.sem.loc, sent)

@@ -15,13 +15,12 @@ SCRATCH = {"X": ("sbuf", [128, 4096], "bfloat16"), "ia": ("sbuf", [128, 128], "i
            "base0": ("sbuf", [128, 64], "float32"), "Q": ("sbuf", [128, 144], "bfloat16"),
            "zmask": ("sbuf", [128, NB], "bfloat16"), "K32": ("sbuf", [128, NT], "float32"), "ks": ("sbuf", [128, 2 * NT], "float32"),
            "SI": ("sbuf", [128, 256], "float32")}
-F32 = ("P", "dhs", "dos", "thr", "m", "t2", "cho", "um", "sc", "P2", "ad", "hsb", "spoh", "kset", "absoh")
+F32 = ("P", "dhs", "Hc", "thr", "m", "s1", "cho", "um", "sc", "P2", "ad", "hsb", "spoh", "kset")
 I32 = ("S", "ci", "ui", "u12", "u5", "gx", "gs", "S2", "fx", "pc", "od2")
 SMALL = {}
-for _n in ("ones", "bt", "BM", "I", "nI", "n8I", "I2", "n3I", "TRI", "TRI16", "Wb", "cm"):
+for _n in ("ones", "bt", "BM", "I", "nI", "n8I", "c91", "c200", "n300", "n3I", "TRI", "TRI16", "Wb"):
     SCRATCH[_n] = ("sbuf", [128, 128], "bfloat16")
-for _n in ("If", "nIf", "If32", "If1184", "o16f"):
-    SCRATCH[_n] = ("sbuf", [128, 128], "float32")
+SCRATCH["o16f"] = ("sbuf", [128, 128], "float32")
 for _t in range(NT):
     SCRATCH["L%d" % _t] = ("sbuf", [128, 256], "float32")
     SCRATCH["Z%d" % _t] = ("sbuf", [128, 384], "bfloat16")
@@ -52,7 +51,7 @@ PS = {}
 for _h in range(NH):
     for _i, _n in enumerate(("dh", "do", "dc", "dhp", "V", "cnt", "cntv", "u")):
         PS[_n, _h] = (2 + _h, _i)
-    for _i, _n in enumerate(("H", "L", "OH", "L2", "Hn", "zd", "cnt2", "hsum")):
+    for _i, _n in enumerate(("H", "L", "OH", "L2", "O1", "zd", "cnt2", "hsum")):
         PS[_n, _h] = (4 + _h, _i)
     for _i, _n in enumerate(("CH", "d", "tmp")):
         PS[_n, _h] = (6, 3 * _h + _i)
@@ -60,12 +59,19 @@ for _h in range(NH):
         PS[_n, _h] = (7, 4 * _h + _i)
 PS["mask", 0] = (6, 6)
 
-CY = 0.83e-3 * 1.25
-PCY = 0.5e-3
+CY = 0.83e-3 * 1.2
+PCY = 0.55 * 1e-3
 GA = 1.6
-BONUS, WINDOW = 2.0, 0.03
-OFFS = {}
-HOP = 3.5
+WAKE, OWN = 0.16, 0.16
+BONUS, WINDOW = 0, 0.005
+OFFS = {'zbuf_1': -2.0, 'ps4:L20': -2.2, 'dhs_1': 1.0, 'ps5:H1': -3.1, 'ps5:L21': -2.0, 'hsb_1': -10.0, 'ps5:OH1': 15.0, 'ps6:tmp1': 11.0,
+        'Hc_1': 8.0, 'od_0.0': -3.0, 'od_1.0': 4.0, 'ps4:OH0': -4.0, 'ps5:hsum1': 14.0, 'ps6:tmp0': -2.0, 'hr_1.0': -2.2, 'send_0_zg': 2.0,
+        'gx_1': 2.5, 'fx_0': 4.0, 'P_0': -11.0, 'zexp_1.0': 10.0, 'u5_0': -2.0, 'acc_0': 5.0, 'ho16_1': -14.0, 'zbuf_0': -10.0, 'S2_0': -2.0,
+        'spoh_1': -8.4, 'm_0': -3.0, 'ps7:incs0': -2.0, 'fx_1': -8.0, 'cabs_1.1': -4.0, 'hr_1.1': -5.6, 'sp_0': 8.0, 'rec_1': -9.0,
+        'zexp_1.1': -9.0, 'hr_0.1': 5.0, 'inc_0': 8.0, 'ps4:H0': 1.5, 'orl_1.0': 3.0, 'cabs_1.0': -5.0, 'ch_0.1': -3.0, 'kset_0': -6.0,
+        'zexp_0.1': -6.4, 'od_1.1': -5.0, 'acc_1': -14.0, 'ps5:L1': -1.6, 'ps5:O11': 10.0, 'dhs_0': 6.0, 'ad_0': -11.0, 'cd_1.1': -7.0,
+        'orl_0.1': 8.0, 'cho_1': 4.0, 'ps7:Gs1': 18.0, 'u16_0': -4.0, 'orl_0.0': -3.0}
+HOP = 5.2
 
 
 def build():
@@ -184,11 +190,6 @@ def build():
     gp = lambda fn, r, w: add("g", 0.5, fn, r, w, sem="qg")
     memset("ones", 1.0, 128)
     gp(lambda g, T: g.affine_select(T.I[:], T.ones[:], [[-1, 128]], OP.is_equal, 0.0, 0, 1), ["ones"], ["I"])
-    act(full("If"), full("I"), AF.Copy, n=128)
-    act(full("nIf"), full("I"), AF.Copy, scale=-1.0, n=128)
-    act(full("If32"), full("I"), AF.Copy, scale=32.0, n=128)
-    act(full("If1184"), full("I"), AF.Copy, scale=1184.0, n=128)
-    memset("cm", -65536.0, 128)
     gp(lambda g, T: g.affine_select(T.bt[:], T.ones[:], [[-16, 8], [0, 16]], OP.is_ge, 0.0, 0, 1), ["ones"], ["bt"])
     gp(lambda g, T: g.affine_select(T.BM[:], T.bt[:], [[16, 8], [0, 16]], OP.is_ge, 0.0, 15, -1), ["bt"], ["BM"])
     gp(lambda g, T: g.affine_select(T.TRI[:], T.BM[:], [[1, 128]], OP.is_gt, 0.0, 0, -1), ["BM"], ["TRI"])
@@ -204,7 +205,9 @@ def build():
     act(full("n8I"), full("I"), AF.Copy, scale=-8192.0, n=128)
     ts(full("TRI16"), full("I"), -16.0, OP.mult, n=128, half=True)
     tt(full("TRI16"), full("TRI16"), full("TRI"), OP.add, n=128)
-    act(full("I2"), full("I"), AF.Copy, scale=2.0, n=128)
+    act(full("c91"), full("I"), AF.Copy, scale=91.0, n=128)
+    act(full("c200"), full("I"), AF.Copy, scale=200.0, n=128)
+    act(full("n300"), full("I"), AF.Copy, scale=-300.0, n=128)
     act(full("n3I"), full("I"), AF.Copy, scale=-3.0, n=128)
     ts(full("Wb"), full("BM"), lambda T: T.wc[:], OP.mult, n=128, half=True, extra=["wc"])
     gp(lambda g, T: g.iota(T.mi[:], [[-1, 64]], 64, 1), [], ["mi"])
@@ -231,23 +234,22 @@ def build():
             z = cols("Z%d" % t, 192 * h, 192 * h + 64, key=zk)
             Iold = cols("Z%d" % t, 192 * h + 64, 192 * h + 128, key=ik)
             Gold = cols("Z%d" % t, 192 * h + 128, 192 * h + 192, key=ik)
-            if t == 0:
-                cm_ = [(full("cm"), cols("ones", 0, 64), 64, 1)]
             if t > 0:
                 add(None, 0.0, None, ["send_%d_%d_L" % (t - 1, h)], [lk], arr="arr_%d_%d_L" % (t, h), lat=HOP)
                 add(None, 0.0, None, ["send_%d_%d_Z" % (t - 1, h)], [zk], arr="arr_%d_%d_Z" % (t, h), lat=HOP)
                 add(None, 0.0, None, ["send_%d_%d_N" % (t - 1, h)], [ik], arr="arr_%d_%d_N" % (t, h), lat=HOP)
             cp(sb("ho16", h), cols("L%d" % t, 128 * h, 128 * h + 128, key=lk), n=128)
             add("a", 64 * CY, lambda g, T, h=h, z=z: g.scalar.activation(T["zbuf_%d" % h][:, 0:NB:16], z[1](T), AF.Copy), [zk, "zbuf_%d" % h], ["zbuf_%d" % h])
-            mm(pk("H", h), [f4("If", LH)])
-            mm(pk("L", h), [f4("If32", LH), f4("If1184", LO)] + cm_)
-            mm(pk("OH", h), [f4("If", LO), f4("nIf", LH)])
-            tt(sb("P", h), LO, pk("H", h), OP.mult)
+            act(sb("Hc", h), LH, AF.Copy, bias=-2048.0)
+            act(pk("O1", h), LO, AF.Copy, bias=32.0)
+            act(pk("L", h), LO, AF.Copy, scale=3232.0, bias=65536.0 - 8388608.0)
+            act(pk("H", h), LH, AF.Copy)
+            tt(sb("P", h), sb("Hc", h), pk("O1", h), OP.mult)
             tt(sb("S", h), sb("P", h), pk("L", h), OP.add)
+            tt(pk("OH", h), LO, pk("H", h), OP.subtract)
             ts(sb("ci", h), sb("S", h), 5, OP.arith_shift_right, 4095, OP.bitwise_and)
             cp(sb("c16", h), sb("ci", h))
-            act(sb("absoh", h), pk("OH", h), AF.Abs)
-            act(sb("set", h), sb("absoh", h), AF.Relu, scale=-1.0, bias=1.0)
+            ts(sb("set", h), pk("OH", h), 0.0, OP.is_equal)
             for p in range(NPC):
                 ze = piece("zexp", h, p)
                 add("v", PCB / 2 * CY, lambda g, T, h=h, p=p: g.vector.tensor_tensor_scan(
@@ -262,28 +264,29 @@ def build():
                 act(piece("ha", h, p), yb, AF.Abs, n=PCB)
             for p in range(NPC):
                 gather_v(piece("od", h, p), lo(p), piece("zexp", h, p), PCB)
-                ts(piece("orl", h, p), piece("od", h, p), 0.0, OP.min, -2.0, OP.mult, n=PCB, half=True)
+                act(piece("orl", h, p), piece("od", h, p), AF.Abs, n=PCB)
             for p in range(NPC):
                 gather_v(piece("cd", h, p), lc(p), piece("zexp", h, p), PCB)
                 act(piece("cabs", h, p), piece("cd", h, p), AF.Abs, n=PCB)
             q = lambda j: ("Q", lambda T, j=j: T.Q[:, 15 - j:143 - j])
             mm(pk("dh", h), [(q(j), col16("ha", h, j), 64, 1) for j in range(16)])
-            mm(pk("do", h), [(q(j), col16(n, h, j), 64, 1) for n in ("od", "orl") for j in range(16)])
+            mm(pk("do", h), [(q(j), col16("orl", h, j), 64, 1) for j in range(16)])
             mm(pk("dc", h), [(q(j), col16("cabs", h, j), 64, 1) for j in range(16)])
             act(sb("dhs", h), pk("dh", h), AF.Copy)
-            act(sb("dos", h), pk("do", h), AF.Copy)
-            mm(pk("dhp", h), [f4("If", sb("dhs", h)), f1("n8I", Gold), f1("n8I", sb("set", h))])
-            tt(sb("thr", h), sb("dos", h), pk("dhp", h), OP.min)
+            mm(pk("dhp", h), [f1("n8I", Gold), f1("n8I", sb("set", h))])
+            tt(sb("thr", h), sb("dhs", h), pk("do", h), OP.min)
+            tt(sb("thr", h), sb("thr", h), pk("dhp", h), OP.add)
             tt(sb("w", h), pk("dc", h), sb("thr", h), OP.is_lt)
             mm(pk("cnt", h), [f1("TRI16", sb("w", h))])
             tt(sb("m", h), sb("dhs", h), pk("dc", h), OP.min)
             tt(sb("rec", h), pk("do", h), sb("m", h), OP.is_le)
             tt(pk("CH", h), sb("ci", h), pk("H", h), OP.subtract)
             tt(pk("tmp", h), sb("rec", h), pk("OH", h), OP.mult)
+            tt(sb("s1", h), LH, pk("tmp", h), OP.add)
             ts(sb("am", h), pk("cnt", h), -13.0, OP.is_lt)
-            tt(sb("t2", h), sb("am", h), pk("CH", h), OP.mult)
-            tt(pk("d", h), sb("t2", h), pk("tmp", h), OP.add)
-            tt(sb("cho", h), LH, pk("d", h), OP.add)
+            tt(pk("d", h), sb("am", h), pk("CH", h), OP.mult)
+            tt(sb("cho", h), sb("s1", h), pk("d", h), OP.add)
+            tt(pk("d", h), sb("cho", h), pk("H", h), OP.subtract)
             cp(sb("ch16", h), sb("cho", h))
             for p in range(NPC):
                 gather_a(piece("ch", h, p), lch(p), PCB)
@@ -312,11 +315,12 @@ def build():
             tt(sb("yv", h), pk("V", h), sb("hsb", h), OP.is_ge)
             mm(pk("cntv", h), [f1("BM", sb("yv", h))])
             ts(sb("acc", h), pk("cntv", h), 9.0, OP.is_ge)
-            mm(pk("incs", h), [f1("I", sb("rec", h)), f1("I", sb("am", h)), f1("I2", sb("set", h)), f1("I", sb("acc", h))])
-            ts(sb("inc", h), pk("incs", h), 2.0, OP.is_lt)
-            mm(pk("In", h), [f1("I", Iold), f1("I", sb("inc", h))])
-            ts(sb("sp", h), pk("In", h), 3.0, OP.is_ge)
+            grow = [f1("c91", sb("rec", h)), f1("c91", sb("am", h)), f1("c200", sb("set", h)), f1("BM", sb("yv", h))]
+            mm(pk("dhp", h), [f1("n300", Iold)] + grow)
+            ts(sb("sp", h), pk("dhp", h), -500.0, OP.is_lt)
             mm(pk("cnt2", h), [f1("TRI", sb("sp", h))])
+            mm(pk("incs", h), grow)
+            ts(sb("inc", h), pk("incs", h), 100.0, OP.is_lt)
             sl, sz = "SL%d" % t, "SZ%d" % t
             sh = "send_%d_%d" % (t, h)
             tt(pk("tmp", h), sb("set", h), pk("H", h), OP.mult)
@@ -329,21 +333,20 @@ def build():
             tt(pk("CH", h), sb("od2", h), pk("CH", h), OP.mult)
             tt(pk("tmp", h), pk("CH", h), sb("spoh", h), OP.subtract)
             tt(pk("d", h), sb("acc", h), pk("d", h), OP.mult)
-            terms = [f4("If32", LO)]
+            act(pk("L2", h), LO, AF.Copy, scale=32.0, bias=-8388608.0)
             if t > 0:
                 act(sb("kset", h), sb("set", h), AF.Identity, scale=lambda T, t=t: T.K32[:, t - 1:t], extra=["K32.%d" % (t - 1)])
-                terms.append(f4("If", sb("kset", h)))
-            mm(pk("L2", h), terms + cm_)
+                tt(pk("L2", h), sb("kset", h), pk("L2", h), OP.add)
             tt(sb("S2", h), sb("P2", h), pk("L2", h), OP.add)
             ts(sb("fx", h), sb("S2", h), 5, OP.arith_shift_right, 4095, OP.bitwise_and)
             tt(cols(sl, cb, cb + 64, key=sh + "_lo"), sb("fx", h), pk("tmp", h), OP.add)
             tt(sb("ad", h), LH, pk("d", h), OP.add)
             tt(cols(sl, ca, ca + 64, key=sh + "_lh"), sb("ad", h), pk("CH", h), OP.add)
             mm(pk("I2", h), [f1("I", Iold), f1("I", sb("inc", h)), f1("n3I", sb("sp", h))])
-            mm(pk("Gs", h), [f1("I", sb("am", h)), f1("I", sb("acc", h)), f1("I2", Gold)])
+            mm(pk("Gs", h), [f1("c91", sb("am", h)), f1("c200", Gold), f1("BM", sb("yv", h))])
             if last:
                 act(cols("SI", 128 * h, 128 * h + 64, key="si%d" % h), pk("I2", h), AF.Copy)
-                ts(cols("SI", 128 * h + 64, 128 * h + 128, key="sg%d" % h), pk("Gs", h), 2.0, OP.is_ge)
+                ts(cols("SI", 128 * h + 64, 128 * h + 128, key="sg%d" % h), pk("Gs", h), 100.0, OP.is_ge)
                 ka, kb = sh + "_lh", sh + "_lo"
                 dma("s", "out%d" % (4 * h), (None, lambda T, h=h: T.yi[:, 64 * h:64 * h + 64]), cols("SI", 128 * h, 128 * h + 64, key="si%d" % h), 2.0)
                 dma("s", "out%d" % (4 * h + 1), (None, lambda T, h=h: T.yg[:, 64 * h:64 * h + 64]), cols("SI", 128 * h + 64, 128 * h + 128, key="sg%d" % h), 2.0)
@@ -351,7 +354,7 @@ def build():
                 dma("s", "out%d" % (4 * h + 3), (None, lambda T, h=h: T.yb[:, 64 * h:64 * h + 64]), cols(sl, cb, cb + 64, key=kb), 2.0)
             else:
                 act(cols(sz, 192 * h + 64, 192 * h + 128, key=sh + "_zi"), pk("I2", h), AF.Copy)
-                ts(cols(sz, 192 * h + 128, 192 * h + 192, key=sh + "_zg"), pk("Gs", h), 2.0, OP.is_ge)
+                ts(cols(sz, 192 * h + 128, 192 * h + 192, key=sh + "_zg"), pk("Gs", h), 100.0, OP.is_ge)
                 mm(pk("zd", h), [f1("I", z), f1("nI", M)])
                 act(cols(sz, 192 * h, 192 * h + 64, key=sh + "_zz"), pk("zd", h), AF.Abs)
                 act(sb("dm", h), sb("acc", h), AF.Copy, accum=cols("ks", 2 * t + h, 2 * t + h + 1, key="ks%d_%d" % (t, h)))
@@ -371,7 +374,7 @@ def opclass(o):
     c = o["w"][0] if o["w"] else ""
     for p in ("l", "z", "ig", "send_", "K32.", "ks"):
         if o["t"] >= 0 and c.startswith(p + str(o["t"])):
-            c = p + c[len(p) + 1:]
+            c = p + c[len(p) + 1:].lstrip("_")
     return c
 
 
@@ -436,13 +439,13 @@ def schedule(gr, offs, bonus, window):
                 s = f
             for b in o["banks"]:
                 for e, j in bank.get(b, {}).items():
-                    if e != q and end[j] + 0.1 > s:
-                        s = end[j] + 0.1
+                    if e != q and end[j] + WAKE > s:
+                        s = end[j] + WAKE
             est[i] = s
             if s < mins.get(q, 1e9):
                 mins[q] = s
         q = min(mins, key=lambda k: mins[k])
-        i = max([k for k in est if ops[k]["q"] == q and est[k] <= mins[q] + window], key=lambda k: pri[k])
+        i = min([k for k in est if ops[k]["q"] == q], key=lambda k: est[k] - window * pri[k])
         o, s = ops[i], est[i]
         for b in o["banks"]:
             for e, j in bank.get(b, {}).items():
@@ -458,7 +461,7 @@ def schedule(gr, offs, bonus, window):
         for k in succ[i]:
             left[k] -= 1
             if left[k] == 0:
-                rdy[k] = max(end[j] + (0.05 if ops[j]["q"] == ops[k]["q"] else 0.1) for j in deps[k])
+                rdy[k] = max(end[j] + (OWN if ops[j]["q"] == ops[k]["q"] else WAKE) for j in deps[k])
     assert len(order) == n
     return deps, order, max(end)
 

import numpy as np
from concourse.mybir import AluOpType as OP, ActivationFunctionType as AF

NT = 5
NH = 2
NPK = 64
NB = 16 * NPK
NPC = 2
PCB = NB // NPC
PCK = NPK // NPC

SCRATCH = {"X": ("sbuf", [128, 4096], "bfloat16"), "ia": ("sbuf", [128, 128], "int32"), "ib": ("sbuf", [128, 128], "int32"),
           "wc": ("sbuf", [128, 1], "bfloat16"), "r32": ("sbuf", [128, 1], "float32"), "ri": ("sbuf", [128, 1], "int32"),
           "rj": ("sbuf", [128, 1], "int32"), "mi": ("sbuf", [128, 64], "int32"), "mj": ("sbuf", [128, 64], "int32"),
           "base0": ("sbuf", [128, 64], "float32"), "Q": ("sbuf", [128, 144], "bfloat16"),
           "zmask": ("sbuf", [128, NB], "bfloat16"), "K32": ("sbuf", [128, NT], "float32"), "ks": ("sbuf", [128, 2 * NT], "float32"),
           "SI": ("sbuf", [128, 256], "float32")}
F32 = ("P", "dhs", "Hc", "thr", "m", "s1", "cho", "um", "sc", "P2", "ad", "hsb", "spoh", "kset")
I32 = ("S", "ci", "ui", "u12", "u5", "gx", "gs", "S2", "fx", "pc", "od2")
SMALL = {}
for _n in ("ones", "bt", "BM", "I", "nI", "n8I", "c91", "c200", "n300", "n3I", "TRI", "TRI16", "Wb"):
    SCRATCH[_n] = ("sbuf", [128, 128], "bfloat16")
SCRATCH["o16f"] = ("sbuf", [128, 128], "float32")
for _t in range(NT):
    SCRATCH["L%d" % _t] = ("sbuf", [128, 256], "float32")
    SCRATCH["Z%d" % _t] = ("sbuf", [128, 384], "bfloat16")
    SCRATCH["SL%d" % _t] = ("sbuf", [128, 256], "float32")
    SCRATCH["SZ%d" % _t] = ("sbuf", [128, 384], "bfloat16")
for _h in range(NH):
    for _n in ("zbuf", "zexp", "hr", "ha", "od", "orl", "cd", "cabs", "ch", "Mf"):
        SCRATCH["%s_%d" % (_n, _h)] = ("sbuf", [128, NB], "bfloat16")
    SCRATCH["ho16_%d" % _h] = ("sbuf", [128, 128], "uint16")
    for _n in ("c16", "ch16"):
        SCRATCH["%s_%d" % (_n, _h)] = ("sbuf", [128, 64], "uint16")
    SCRATCH["u16_%d" % _h] = ("sbuf", [128, 4], "uint16")
    for _i, _n in enumerate(F32):
        SMALL["%s_%d" % (_n, _h)] = ("F_%d" % _h, 64 * _i)
    SCRATCH["F_%d" % _h] = ("sbuf", [128, 64 * len(F32)], "float32")
    for _i, _n in enumerate(I32):
        SMALL["%s_%d" % (_n, _h)] = ("J_%d" % _h, 64 * _i)
    SCRATCH["J_%d" % _h] = ("sbuf", [128, 64 * len(I32)], "int32")
    for _n in ("set", "rec", "w", "am", "yv", "acc", "inc", "sp", "dm"):
        SCRATCH["%s_%d" % (_n, _h)] = ("sbuf", [128, 64], "bfloat16")
for _b in range(8):
    SCRATCH["ps%d" % _b] = ("psum", [128, 512], "float32")

SEMAPHORES = ["qv", "qa", "qt", "qg", "loc"] + ["in%d" % _i for _i in range(7)] + ["out%d" % _i for _i in range(8)] + \
    ["arr_%d_%d_%s" % (_t, _h, _k) for _t in range(1, NT) for _h in range(NH) for _k in "LZN"]

PS = {}
for _h in range(NH):
    for _i, _n in enumerate(("dh", "do", "dc", "dhp", "V", "cnt", "cntv", "u")):
        PS[_n, _h] = (2 + _h, _i)
    for _i, _n in enumerate(("H", "L", "OH", "L2", "O1", "zd", "cnt2", "hsum")):
        PS[_n, _h] = (4 + _h, _i)
    for _i, _n in enumerate(("CH", "d", "tmp")):
        PS[_n, _h] = (6, 3 * _h + _i)
    for _i, _n in enumerate(("incs", "Gs", "In", "I2")):
        PS[_n, _h] = (7, 4 * _h + _i)
PS["mask", 0] = (6, 6)

CY = 0.83e-3 * 1.2
PCY = 0.55 * 1e-3
GA = 1.6
WAKE, OWN = 0.16, 0.16
BONUS, WINDOW = 0, 0.005
OFFS = {'zbuf_1': -2.0, 'ps4:L20': -2.2, 'dhs_1': 1.0, 'ps5:H1': -3.1, 'ps5:L21': -2.0, 'hsb_1': -10.0, 'ps5:OH1': 15.0, 'ps6:tmp1': 11.0,
        'Hc_1': 8.0, 'od_0.0': -3.0, 'od_1.0': 4.0, 'ps4:OH0': -4.0, 'ps5:hsum1': 14.0, 'ps6:tmp0': -2.0, 'hr_1.0': -2.2, 'send_0_zg': 2.0,
        'gx_1': 2.5, 'fx_0': 4.0, 'P_0': -11.0, 'zexp_1.0': 10.0, 'u5_0': -2.0, 'acc_0': 5.0, 'ho16_1': -14.0, 'zbuf_0': -10.0, 'S2_0': -2.0,
        'spoh_1': -8.4, 'm_0': -3.0, 'ps7:incs0': -2.0, 'fx_1': -8.0, 'cabs_1.1': -4.0, 'hr_1.1': -5.6, 'sp_0': 8.0, 'rec_1': -9.0,
        'zexp_1.1': -9.0, 'hr_0.1': 5.0, 'inc_0': 8.0, 'ps4:H0': 1.5, 'orl_1.0': 3.0, 'cabs_1.0': -5.0, 'ch_0.1': -3.0, 'kset_0': -6.0,
        'zexp_0.1': -6.4, 'od_1.1': -5.0, 'acc_1': -14.0, 'ps5:L1': -1.6, 'ps5:O11': 10.0, 'dhs_0': 6.0, 'ad_0': -11.0, 'cd_1.1': -7.0,
        'orl_0.1': 8.0, 'cho_1': 4.0, 'ps7:Gs1': 18.0, 'u16_0': -4.0, 'orl_0.0': -3.0}
HOP = 5.2


def build():
    ops = []
    cur = {"h": None, "t": -1}

    def add(q, cost, fn, r, w, **kw):
        ops.append(dict(q=q, cost=cost, fn=fn, r=list(r), w=list(w), h=cur["h"], t=cur["t"], **kw))

    def ps(name, h, T):
        b, i = PS[name, h]
        return T["ps%d" % b][:, 64 * i:64 * i + 64]

    def full(name):
        return (name, lambda T: T[name][:])

    def pk(name, h):
        return ("ps%d:%s%d" % (PS[name, h][0], name, h), lambda T: ps(name, h, T))

    def sb(name, h):
        n = "%s_%d" % (name, h)
        if n in SMALL:
            b, c = SMALL[n]
            return (n, lambda T: T[b][:, c:c + 64])
        return (n, lambda T: T[n][:])

    def cols(name, a, b, step=1, key=None):
        return (key or name, lambda T: T[name][:, a:b:step] if step != 1 else T[name][:, a:b])

    def inps(x):
        return x[0].startswith("ps")

    def tt(out, a, b, op, n=64):
        c = max(64, n * (1 if inps(a) or inps(b) else 2))
        add("v", c * CY, lambda g, T: g.vector.tensor_tensor(out[1](T), a[1](T), b[1](T), op), [a[0], b[0]], [out[0]])

    def ts(out, a, s1, op0, s2=None, op1=None, n=64, half=False, extra=()):
        c = max(64, n * (0.5 if half else 1))

        def fn(g, T):
            sc = s1(T) if callable_(s1) else s1
            if op1 is None:
                return g.vector.tensor_scalar(out[1](T), a[1](T), sc, None, op0)
            return g.vector.tensor_scalar(out[1](T), a[1](T), sc, s2, op0, op1)
        add("v", c * CY, fn, [a[0]] + list(extra), [out[0]])

    def callable_(x):
        return not isinstance(x, (int, float))

    def cp(out, a, n=64):
        add("v", max(64, n) * CY, lambda g, T: g.vector.tensor_copy(out[1](T), a[1](T)), [a[0]], [out[0]])

    def act(out, a, func, scale=1.0, bias=0.0, n=64, extra=(), accum=None):
        def fn(g, T):
            kw = {}
            if scale != 1.0 or callable_(scale):
                kw["scale"] = scale(T) if callable_(scale) else scale
            if bias != 0.0:
                kw["bias"] = bias
            if accum is not None:
                kw["accum_out"] = accum[1](T)
            return g.scalar.activation(out[1](T), a[1](T), func, **kw)
        add("a", max(64, n) * CY + 0.02, fn, [a[0]] + list(extra), [out[0]] + ([accum[0]] if accum is not None else []))

    def mm(out, terms):
        def fn(g, T):
            r = None
            for k, (l, x, n, f) in enumerate(terms):
                r = g.tensor.matmul(out[1](T), l[1](T), x[1](T), k == 0, k == len(terms) - 1)
            return r
        keys = []
        for l, x, n, f in terms:
            for y in (l, x):
                for kk in (y[0] if isinstance(y[0], (list, tuple)) else [y[0]]):
                    if kk not in keys:
                        keys.append(kk)
        add("t", sum(max(64, n) * f for l, x, n, f in terms) * PCY, fn, keys, [out[0]])

    def f1(l, x, n=64):
        return (full(l), x, n, 1)

    def f4(l, x, n=64):
        return (full(l), x, n, 4)

    def gather_v(out, lst, z, n):
        add("v", 0.05 + n * GA * CY, lambda g, T: g.vector.tensor_tensor(out[1](T), T.X[:, 0:4096].indirect(lst[1](T)), z[1](T), OP.subtract),
            ["X0", "X1", lst[0], z[0]], [out[0]])

    def gather_a(out, lst, n):
        add("a", 0.065 + n * GA * CY, lambda g, T: g.scalar.activation(out[1](T), T.X[:, 0:4096].indirect(lst[1](T)), AF.Copy),
            ["X0", "X1", lst[0]], [out[0]])

    def memset(name, val, n, sl=None, key=None):
        add("v", max(64, n) * CY, lambda g, T: g.vector.memset(sl(T) if sl is not None else T[name][:], val), [], [key or name])

    def dma(q, sem, out, src, cost):
        def fn(g, T):
            return (g.sync if q == "s" else g.scalar).dma_start(out[1](T), src[1](T))
        add(q, 0.1, fn, [src[0]] if src[0] else [], [out[0]], sem=sem, lat=cost)

    def piece(name, h, p):
        n = "%s_%d" % (name, h)
        return ("%s.%d" % (n, p), lambda T: T[n][:, p * PCB:(p + 1) * PCB])

    def col16(name, h, j):
        n = "%s_%d" % (name, h)
        return (["%s.%d" % (n, p) for p in range(NPC)], lambda T: T[n][:, j:NB:16])

    dma("s", "in0", full("ia"), (None, lambda T: T.ba[:]), 2.0)
    dma("a", "in1", full("ib"), (None, lambda T: T.bb[:]), 2.0)
    dma("s", "in2", ("X0", lambda T: T.X[:, 0:2048]), (None, lambda T: T.xt[:, 0:2048]), 5.0)
    dma("a", "in3", ("X1", lambda T: T.X[:, 2048:4096]), (None, lambda T: T.xt[:, 2048:4096]), 5.0)
    for h in range(NH):
        dma("s", "in%d" % (4 + h), cols("Z0", 192 * h, 192 * h + 64, key="z0_%d" % h), (None, lambda T, h=h: T.zp[:, 64 * h:64 * h + 64]), 2.2)
    dma("s", "in6", full("wc"), (None, lambda T: T.wl[:]), 2.2)
    gp = lambda fn, r, w: add("g", 0.5, fn, r, w, sem="qg")
    memset("ones", 1.0, 128)
    gp(lambda g, T: g.affine_select(T.I[:], T.ones[:], [[-1, 128]], OP.is_equal, 0.0, 0, 1), ["ones"], ["I"])
    gp(lambda g, T: g.affine_select(T.bt[:], T.ones[:], [[-16, 8], [0, 16]], OP.is_ge, 0.0, 0, 1), ["ones"], ["bt"])
    gp(lambda g, T: g.affine_select(T.BM[:], T.bt[:], [[16, 8], [0, 16]], OP.is_ge, 0.0, 15, -1), ["bt"], ["BM"])
    gp(lambda g, T: g.affine_select(T.TRI[:], T.BM[:], [[1, 128]], OP.is_gt, 0.0, 0, -1), ["BM"], ["TRI"])
    for h in range(NH):
        memset("zbuf_%d" % h, 0.0, NB // 2)
        memset("Z0", 0.0, 64, sl=lambda T, h=h: T.Z0[:, 192 * h + 64:192 * h + 192], key="ig0_%d" % h)
    memset("zmask", 1.0, NB // 2)
    memset("zmask", 0.0, 64, sl=lambda T: T.zmask[:, 0:NB:16])
    ops[-1]["r"].append("zmask")
    memset("Q", 0.0, 144)
    add("v", 64 * CY, lambda g, T: g.vector.tensor_copy(T.Q[:, 15:143:16], T.BM[:, 0:128:16]), ["BM", "Q"], ["Q"])
    act(full("nI"), full("I"), AF.Copy, scale=-1.0, n=128)
    act(full("n8I"), full("I"), AF.Copy, scale=-8192.0, n=128)
    ts(full("TRI16"), full("I"), -16.0, OP.mult, n=128, half=True)
    tt(full("TRI16"), full("TRI16"), full("TRI"), OP.add, n=128)
    act(full("c91"), full("I"), AF.Copy, scale=91.0, n=128)
    act(full("c200"), full("I"), AF.Copy, scale=200.0, n=128)
    act(full("n300"), full("I"), AF.Copy, scale=-300.0, n=128)
    act(full("n3I"), full("I"), AF.Copy, scale=-3.0, n=128)
    ts(full("Wb"), full("BM"), lambda T: T.wc[:], OP.mult, n=128, half=True, extra=["wc"])
    gp(lambda g, T: g.iota(T.mi[:], [[-1, 64]], 64, 1), [], ["mi"])
    gp(lambda g, T: g.iota(T.ri[:], [[0, 1]], 0, 1), [], ["ri"])
    gp(lambda g, T: g.iota(T.base0[:], [[512, 4], [0, 16]], 0, 0, allow_small_or_imprecise_dtypes=True), [], ["base0"])
    ts(full("mj"), full("mi"), 15, OP.bitwise_and)
    ts(pk("mask", 0), full("mj"), 0.0, OP.is_equal)
    ts(full("rj"), full("ri"), 15, OP.bitwise_and)
    ts(full("r32"), full("rj"), 32.0, OP.mult)
    memset("o16f", 0.0625, 128)

    for h in range(NH):
        cp(cols("L0", 128 * h, 128 * h + 64, key="l0_%d" % h), cols("ia", 64 * h, 64 * h + 64))
        cp(cols("L0", 128 * h + 64, 128 * h + 128, key="l0_%d" % h), cols("ib", 64 * h, 64 * h + 64))

    for t in range(NT):
        last = t == NT - 1
        scat = []
        for h in range(NH):
            cur["h"], cur["t"] = h, t
            lk, zk, ik = "l%d_%d" % (t, h), "z%d_%d" % (t, h), "ig%d_%d" % (t, h)
            ca, cb = 128 * h + 64 * (t % 2), 128 * h + 64 * (1 - t % 2)
            LH, LO = cols("L%d" % t, ca, ca + 64, key=lk), cols("L%d" % t, cb, cb + 64, key=lk)
            z = cols("Z%d" % t, 192 * h, 192 * h + 64, key=zk)
            Iold = cols("Z%d" % t, 192 * h + 64, 192 * h + 128, key=ik)
            Gold = cols("Z%d" % t, 192 * h + 128, 192 * h + 192, key=ik)
            if t > 0:
                add(None, 0.0, None, ["send_%d_%d_L" % (t - 1, h)], [lk], arr="arr_%d_%d_L" % (t, h), lat=HOP)
                add(None, 0.0, None, ["send_%d_%d_Z" % (t - 1, h)], [zk], arr="arr_%d_%d_Z" % (t, h), lat=HOP)
                add(None, 0.0, None, ["send_%d_%d_N" % (t - 1, h)], [ik], arr="arr_%d_%d_N" % (t, h), lat=HOP)
            cp(sb("ho16", h), cols("L%d" % t, 128 * h, 128 * h + 128, key=lk), n=128)
            add("a", 64 * CY, lambda g, T, h=h, z=z: g.scalar.activation(T["zbuf_%d" % h][:, 0:NB:16], z[1](T), AF.Copy), [zk, "zbuf_%d" % h], ["zbuf_%d" % h])
            act(sb("Hc", h), LH, AF.Copy, bias=-2048.0)
            act(pk("O1", h), LO, AF.Copy, bias=32.0)
            act(pk("L", h), LO, AF.Copy, scale=3232.0, bias=65536.0 - 8388608.0)
            act(pk("H", h), LH, AF.Copy)
            tt(sb("P", h), sb("Hc", h), pk("O1", h), OP.mult)
            tt(sb("S", h), sb("P", h), pk("L", h), OP.add)
            tt(pk("OH", h), LO, pk("H", h), OP.subtract)
            ts(sb("ci", h), sb("S", h), 5, OP.arith_shift_right, 4095, OP.bitwise_and)
            cp(sb("c16", h), sb("ci", h))
            ts(sb("set", h), pk("OH", h), 0.0, OP.is_equal)
            for p in range(NPC):
                ze = piece("zexp", h, p)
                add("v", PCB / 2 * CY, lambda g, T, h=h, p=p: g.vector.tensor_tensor_scan(
                    T["zexp_%d" % h][:, p * PCB:(p + 1) * PCB], T.zmask[:, 0:PCB], T["zbuf_%d" % h][:, p * PCB:(p + 1) * PCB], 0.0, OP.mult, OP.add),
                    ["zmask", "zbuf_%d" % h], [ze[0]])
            lst = lambda name, a, h=h: (lambda p: ("%s_%d" % (name, h), lambda T: T["%s_%d" % (name, h)][:, a + p * PCK:a + (p + 1) * PCK]))
            lh, lo, lc, lch = lst("ho16", 64 * (t % 2)), lst("ho16", 64 * (1 - t % 2)), lst("c16", 0), lst("ch16", 0)
            for p in range(NPC):
                gather_a(piece("hr", h, p), lh(p), PCB)
                yb = ("ps%d:y" % p, lambda T, p=p: T["ps%d" % p][:, 0:PCB])
                mm(yb, [f1("I", piece("hr", h, p), PCB), f1("nI", piece("zexp", h, p), PCB)])
                act(piece("ha", h, p), yb, AF.Abs, n=PCB)
            for p in range(NPC):
                gather_v(piece("od", h, p), lo(p), piece("zexp", h, p), PCB)
                act(piece("orl", h, p), piece("od", h, p), AF.Abs, n=PCB)
            for p in range(NPC):
                gather_v(piece("cd", h, p), lc(p), piece("zexp", h, p), PCB)
                act(piece("cabs", h, p), piece("cd", h, p), AF.Abs, n=PCB)
            q = lambda j: ("Q", lambda T, j=j: T.Q[:, 15 - j:143 - j])
            mm(pk("dh", h), [(q(j), col16("ha", h, j), 64, 1) for j in range(16)])
            mm(pk("do", h), [(q(j), col16("orl", h, j), 64, 1) for j in range(16)])
            mm(pk("dc", h), [(q(j), col16("cabs", h, j), 64, 1) for j in range(16)])
            act(sb("dhs", h), pk("dh", h), AF.Copy)
            mm(pk("dhp", h), [f1("n8I", Gold), f1("n8I", sb("set", h))])
            tt(sb("thr", h), sb("dhs", h), pk("do", h), OP.min)
            tt(sb("thr", h), sb("thr", h), pk("dhp", h), OP.add)
            tt(sb("w", h), pk("dc", h), sb("thr", h), OP.is_lt)
            mm(pk("cnt", h), [f1("TRI16", sb("w", h))])
            tt(sb("m", h), sb("dhs", h), pk("dc", h), OP.min)
            tt(sb("rec", h), pk("do", h), sb("m", h), OP.is_le)
            tt(pk("CH", h), sb("ci", h), pk("H", h), OP.subtract)
            tt(pk("tmp", h), sb("rec", h), pk("OH", h), OP.mult)
            tt(sb("s1", h), LH, pk("tmp", h), OP.add)
            ts(sb("am", h), pk("cnt", h), -13.0, OP.is_lt)
            tt(pk("d", h), sb("am", h), pk("CH", h), OP.mult)
            tt(sb("cho", h), sb("s1", h), pk("d", h), OP.add)
            tt(pk("d", h), sb("cho", h), pk("H", h), OP.subtract)
            cp(sb("ch16", h), sb("cho", h))
            for p in range(NPC):
                gather_a(piece("ch", h, p), lch(p), PCB)
                add("v", PCB / 2 * CY, lambda g, T, h=h, p=p: g.vector.tensor_tensor_scan(
                    T["Mf_%d" % h][:, p * PCB:(p + 1) * PCB], T.zmask[:, 0:PCB], T["ch_%d" % h][:, p * PCB:(p + 1) * PCB], 0.0, OP.mult, OP.max),
                    ["zmask", "ch_%d.%d" % (h, p)], ["Mf_%d.%d" % (h, p)])
            M = (["Mf_%d.%d" % (h, p) for p in range(NPC)], lambda T, h=h: T["Mf_%d" % h][:, 15:NB:16])
            mm(pk("u", h), [f1("Wb", M)])
            cp(sb("ui", h), pk("u", h))
            if not last:
                ts(sb("u5", h), sb("ui", h), 31, OP.bitwise_and)
                tt(sb("um", h), sb("u5", h), pk("mask", 0), OP.mult)
                add("v", 64 * CY, lambda g, T, sc=sb("sc", h)[1], um=sb("um", h)[1]: g.vector.tensor_tensor_scan(
                    sc(T), T.base0[:], um(T), 0.0, OP.max, OP.add), ["base0", "um_%d" % h], ["sc_%d" % h])
                fb, fc = SMALL["sc_%d" % h]
                ts(sb("u16", h), ("sc_%d" % h, lambda T, fb=fb, fc=fc: T[fb][:, fc + 15:fc + 64:16]), lambda T: T.r32[:], OP.add, extra=["r32"])
                win = lambda T, h=h: T.X[:, 2048 * h:2048 * h + 2048].indirect(T["u16_%d" % h][:, 0:4])
                add("v", 0.05 + 64 * GA * CY, lambda g, T, gx=sb("gx", h)[1], win=win, M=M: g.vector.tensor_tensor(gx(T), win(T), M[1](T), OP.add),
                    ["X%d" % h, "u16_%d" % h] + M[0], ["gx_%d" % h])
                ts(sb("gs", h), sb("gx", h), 1, OP.arith_shift_right)
                scat.append(("v", 0.05 + 64 * 4 * CY, lambda g, T, gs=sb("gs", h)[1], win=win: g.vector.tensor_copy(win(T), gs(T)),
                             ["gs_%d" % h, "u16_%d" % h, "X%d" % h], ["X%d" % h]))
            mm(pk("hsum", h), [(full("I"), col16("hr", h, j), 64, 1) for j in range(16)])
            act(sb("hsb", h), pk("hsum", h), AF.Copy)
            mm(pk("V", h), [(full("I"), col16("ch", h, j), 64, 1) for j in range(16)])
            tt(sb("yv", h), pk("V", h), sb("hsb", h), OP.is_ge)
            mm(pk("cntv", h), [f1("BM", sb("yv", h))])
            ts(sb("acc", h), pk("cntv", h), 9.0, OP.is_ge)
            grow = [f1("c91", sb("rec", h)), f1("c91", sb("am", h)), f1("c200", sb("set", h)), f1("BM", sb("yv", h))]
            mm(pk("dhp", h), [f1("n300", Iold)] + grow)
            ts(sb("sp", h), pk("dhp", h), -500.0, OP.is_lt)
            mm(pk("cnt2", h), [f1("TRI", sb("sp", h))])
            mm(pk("incs", h), grow)
            ts(sb("inc", h), pk("incs", h), 100.0, OP.is_lt)
            sl, sz = "SL%d" % t, "SZ%d" % t
            sh = "send_%d_%d" % (t, h)
            tt(pk("tmp", h), sb("set", h), pk("H", h), OP.mult)
            ts(sb("u12", h), sb("ui", h), 4095, OP.bitwise_and)
            tt(sb("P2", h), sb("u12", h), pk("tmp", h), OP.mult)
            tt(sb("spoh", h), sb("sp", h), pk("OH", h), OP.mult)
            tt(pk("CH", h), sb("sp", h), pk("CH", h), OP.mult)
            cp(sb("pc", h), pk("cnt2", h))
            ts(sb("od2", h), sb("pc", h), 1, OP.bitwise_and)
            tt(pk("CH", h), sb("od2", h), pk("CH", h), OP.mult)
            tt(pk("tmp", h), pk("CH", h), sb("spoh", h), OP.subtract)
            tt(pk("d", h), sb("acc", h), pk("d", h), OP.mult)
            act(pk("L2", h), LO, AF.Copy, scale=32.0, bias=-8388608.0)
            if t > 0:
                act(sb("kset", h), sb("set", h), AF.Identity, scale=lambda T, t=t: T.K32[:, t - 1:t], extra=["K32.%d" % (t - 1)])
                tt(pk("L2", h), sb("kset", h), pk("L2", h), OP.add)
            tt(sb("S2", h), sb("P2", h), pk("L2", h), OP.add)
            ts(sb("fx", h), sb("S2", h), 5, OP.arith_shift_right, 4095, OP.bitwise_and)
            tt(cols(sl, cb, cb + 64, key=sh + "_lo"), sb("fx", h), pk("tmp", h), OP.add)
            tt(sb("ad", h), LH, pk("d", h), OP.add)
            tt(cols(sl, ca, ca + 64, key=sh + "_lh"), sb("ad", h), pk("CH", h), OP.add)
            mm(pk("I2", h), [f1("I", Iold), f1("I", sb("inc", h)), f1("n3I", sb("sp", h))])
            mm(pk("Gs", h), [f1("c91", sb("am", h)), f1("c200", Gold), f1("BM", sb("yv", h))])
            if last:
                act(cols("SI", 128 * h, 128 * h + 64, key="si%d" % h), pk("I2", h), AF.Copy)
                ts(cols("SI", 128 * h + 64, 128 * h + 128, key="sg%d" % h), pk("Gs", h), 100.0, OP.is_ge)
                ka, kb = sh + "_lh", sh + "_lo"
                dma("s", "out%d" % (4 * h), (None, lambda T, h=h: T.yi[:, 64 * h:64 * h + 64]), cols("SI", 128 * h, 128 * h + 64, key="si%d" % h), 2.0)
                dma("s", "out%d" % (4 * h + 1), (None, lambda T, h=h: T.yg[:, 64 * h:64 * h + 64]), cols("SI", 128 * h + 64, 128 * h + 128, key="sg%d" % h), 2.0)
                dma("s", "out%d" % (4 * h + 2), (None, lambda T, h=h: T.ya[:, 64 * h:64 * h + 64]), cols(sl, ca, ca + 64, key=ka), 2.0)
                dma("s", "out%d" % (4 * h + 3), (None, lambda T, h=h: T.yb[:, 64 * h:64 * h + 64]), cols(sl, cb, cb + 64, key=kb), 2.0)
            else:
                act(cols(sz, 192 * h + 64, 192 * h + 128, key=sh + "_zi"), pk("I2", h), AF.Copy)
                ts(cols(sz, 192 * h + 128, 192 * h + 192, key=sh + "_zg"), pk("Gs", h), 100.0, OP.is_ge)
                mm(pk("zd", h), [f1("I", z), f1("nI", M)])
                act(cols(sz, 192 * h, 192 * h + 64, key=sh + "_zz"), pk("zd", h), AF.Abs)
                act(sb("dm", h), sb("acc", h), AF.Copy, accum=cols("ks", 2 * t + h, 2 * t + h + 1, key="ks%d_%d" % (t, h)))
                add("g", 0.3, None, [sh + "_zz"], [sh + "_Z"], send=(t, h, "Z"))
                add("g", 0.3, None, [sh + "_zi", sh + "_zg"], [sh + "_N"], send=(t, h, "N"))
                add("g", 0.3, None, [sh + "_lo", sh + "_lh"], [sh + "_L"], send=(t, h, "L"))
        for x in scat:
            add(*x)
        if not last:
            kp = ("ps4:zd0", lambda T: T.ps4[:, 320:321])
            mm(kp, [f4("o16f", cols("ks", 2 * t + h, 2 * t + h + 1, key="ks%d_%d" % (t, h)), 1) for h in range(NH)])
            act(cols("K32", t, t + 1, key="K32.%d" % t), kp, AF.Copy, scale=-32.0, bias=32768.0)
    return ops


def opclass(o):
    c = o["w"][0] if o["w"] else ""
    for p in ("l", "z", "ig", "send_", "K32.", "ks"):
        if o["t"] >= 0 and c.startswith(p + str(o["t"])):
            c = p + c[len(p) + 1:].lstrip("_")
    return c


def graph():
    ops = build()
    n = len(ops)
    deps = [set() for _ in range(n)]
    lastw, readers = {}, {}

    def keys(l):
        out = []
        for k in l:
            out += keys(k) if isinstance(k, (list, tuple)) else ([k] if k else [])
        return out
    for i, o in enumerate(ops):
        o["r"], o["w"] = keys(o["r"]), keys(o["w"])
        for k in o["r"]:
            if k in lastw:
                deps[i].add(lastw[k])
        for k in o["w"]:
            if k in lastw:
                deps[i].add(lastw[k])
            deps[i].update(readers.get(k, ()))
        for k in o["r"]:
            readers.setdefault(k, []).append(i)
        for k in o["w"]:
            lastw[k] = i
            readers[k] = []
        deps[i].discard(i)
        o["banks"] = sorted(set(k.split(":")[0] for k in o["r"] + o["w"] if k.startswith("ps")))
        o["cls"] = opclass(o)
    succ = [[] for _ in range(n)]
    for i in range(n):
        for j in deps[i]:
            succ[j].append(i)
    pri = [0.0] * n
    for i in range(n - 1, -1, -1):
        o = ops[i]
        pri[i] = o["cost"] + o.get("lat", 0.0) + 0.08 + max([pri[s] for s in succ[i]] or [0.0])
    return ops, deps, succ, pri


def schedule(gr, offs, bonus, window):
    ops, deps, succ, pri = gr
    n = len(ops)
    deps = [set(d) for d in deps]
    pri = [pri[i] + (bonus if ops[i]["h"] == 0 else 0.0) + offs.get(ops[i]["cls"], 0.0) for i in range(n)]
    left = [len(d) for d in deps]
    end = [0.0] * n
    free, bank, order = {}, {}, []
    rdy = {}
    for i in range(n):
        if left[i] == 0:
            rdy[i] = 0.0
    while rdy:
        est, mins = {}, {}
        for i, s in rdy.items():
            o = ops[i]
            q = o["q"]
            f = free.get(q, 0.0) if q else 0.0
            if f > s:
                s = f
            for b in o["banks"]:
                for e, j in bank.get(b, {}).items():
                    if e != q and end[j] + WAKE > s:
                        s = end[j] + WAKE
            est[i] = s
            if s < mins.get(q, 1e9):
                mins[q] = s
        q = min(mins, key=lambda k: mins[k])
        i = min([k for k in est if ops[k]["q"] == q], key=lambda k: est[k] - window * pri[k])
        o, s = ops[i], est[i]
        for b in o["banks"]:
            for e, j in bank.get(b, {}).items():
                if e != q:
                    deps[i].add(j)
            bank.setdefault(b, {})[q] = i
        if q:
            free[q] = s + o["cost"]
        end[i] = s + o["cost"] + o.get("lat", 0.0)
        o["start"] = s
        order.append(i)
        del rdy[i]
        for k in succ[i]:
            left[k] -= 1
            if left[k] == 0:
                rdy[k] = max(end[j] + (OWN if ops[j]["q"] == ops[k]["q"] else WAKE) for j in deps[k])
    assert len(order) == n
    return deps, order, max(end)


def plan(offs=None, bonus=None, window=None):
    gr = graph()
    ops = gr[0]
    deps, order, span = schedule(gr, OFFS if offs is None else offs, BONUS if bonus is None else bonus, WINDOW if window is None else window)
    count = {}
    for i in order:
        o = ops[i]
        if o.get("sem", "").startswith(("in", "out")):
            o["ev"] = (o["sem"], 16)
        elif "arr" in o:
            o["ev"] = (o["arr"], None)
        elif "send" in o:
            o["ev"] = None
        else:
            s = "q" + o["q"]
            count[s] = count.get(s, 0) + 1
            o["ev"] = (s, count[s])
    return ops, deps, order, count, span


_PLAN = []


def rank_program(g, core, T, topo):
    rank = T.rank_of(core)
    if rank is None:
        return
    if not _PLAN:
        _PLAN.append(plan())
    ops, deps, order, count, _ = _PLAN[0]
    n = len(T.cores)
    nxt, prv = T.cores[(rank + 1) % n], T.cores[(rank - 1) % n]

    def engines(a, b):
        return topo.engines(a, b)
    mask = topo.mask(core, nxt)
    n_in, n_out = len(engines(prv, core)), len(engines(core, nxt))
    rid, pid = topo.addr(nxt)[:2]
    queues = {"v": g.vector, "a": g.scalar, "t": g.tensor, "g": g, "s": g.sync}
    seen = {}
    sent = 0
    for i in order:
        o = ops[i]
        if o["q"] is None:
            continue
        q = queues[o["q"]]
        need = {}
        for j in deps[i]:
            ev = ops[j]["ev"]
            if ev is not None:
                need[ev[0]] = max(need.get(ev[0], 0), n_in if ev[1] is None else ev[1])
        for s in sorted(need):
            if seen.get((o["q"], s), 0) < need[s]:
                q.wait_ge(T.sem[s], need[s])
                seen[o["q"], s] = need[s]
        if "send" in o:
            t, h, k = o["send"]
            a, b, w = {"L": (128 * h, 128 * h + 128, "L"), "Z": (192 * h, 192 * h + 64, "Z"), "N": (192 * h + 64, 192 * h + 192, "Z")}[k]
            g.remote_dma(T["%s%d" % (w, t + 1)][:, a:b], T["S%s%d" % (w, t)][:, a:b], T.sem["arr_%d_%d_%s" % (t + 1, h, k)], T.sem.loc, pid, rid, mask)
            sent += n_out
            continue
        r = o["fn"](g, T)
        r.then_inc(T.sem[o["ev"][0]], 16 if o["ev"][0].startswith(("in", "out")) else 1)
    for s in sorted(count):
        g.wait_ge(T.sem[s], count[s])
    for k in range(8):
        g.wait_ge(T.sem["out%d" % k], 16)
    g.wait_ge(T.sem.loc, sent)
